import numpy as np
import ml_dtypes


def mxq(x, axis, fmt="e4m3"):
    dtype, down = {"e4m3": (ml_dtypes.float8_e4m3fn, 7), "e5m2": (ml_dtypes.float8_e5m2, 14)}[fmt]
    v = np.moveaxis(np.asarray(x, np.float32).astype(ml_dtypes.bfloat16).astype(np.float64), axis, -1)
    blocks = v.reshape(v.shape[:-1] + (-1, 32))
    amax = np.abs(blocks).max(-1, keepdims=True)
    byte = np.maximum(np.where(amax > 0, np.frexp(amax)[1] - 1 + 127, 0) - down, 1)
    scale = np.exp2(byte - 127.0)
    codes = (blocks / scale).astype(np.float32).astype(dtype).astype(np.float64)
    return np.moveaxis((codes * scale).reshape(v.shape), -1, axis)


WIDE = False


def mx_kscale(k):
    if not WIDE:
        return np.ones(k)
    levels = np.array([10, -10, 5, -5, 0])
    if k % 512:
        return np.exp2(np.random.permutation(np.resize(levels, k // 32))).repeat(32)
    a = np.empty((k // 512, 16))
    for p in range(k // 512):
        a[p, :8] = np.random.permutation(np.resize(levels, 8))
        for g in range(8):
            far = levels[np.abs(levels - a[p, g]) >= 10]
            a[p, g + 8] = far[np.random.randint(len(far))]
    return np.exp2(a.ravel()).repeat(32)


def f64(x):
    return np.asarray(x).astype(np.float64)


def striped(idx):
    return np.tile(np.asarray(idx).reshape(-1, 16).T, (8, 1)).astype(np.uint16)


def unstriped(offs):
    return offs[:16].T.reshape(-1).astype(np.int64)


def striped8(idx):
    return np.asarray(idx).reshape(8, -1, 16).transpose(0, 2, 1).reshape(128, -1).astype(np.uint16)


def unstriped8(offs):
    return offs.reshape(8, 16, -1).transpose(0, 2, 1).reshape(8, -1).astype(np.int64)


def pick8(x, idx, run):
    r = np.arange(len(x))
    return x[r[:, None], idx[r % (8 * run) // run]]


E2M1 = np.array([0.0, 0.5, 1.0, 1.5, 2.0, 3.0, 4.0, 6.0, -0.0, -0.5, -1.0, -1.5, -2.0, -3.0, -4.0, -6.0])


def pack_weight(w, fmt):
    k, n = w.shape
    w = f64(np.asarray(w, np.float32).astype(ml_dtypes.bfloat16)).reshape(k // 32, 32, n)
    amax = np.abs(w).max(1)
    if fmt == "e4m3":
        byte = np.frexp(amax)[1] - 1 + 127 - 7
    else:
        mant, ex = np.frexp(amax / 6.0)
        byte = np.where(mant > 0.5, ex, ex - 1) + 127
    byte = np.clip(np.where(amax > 0, byte, 1), 1, 254)
    scaled = (w * np.exp2(127.0 - byte)[:, None, :]).reshape(k, n).astype(np.float32)
    by_word = np.ascontiguousarray(scaled.reshape(k // 512, 128, 4, n).transpose(0, 1, 3, 2))
    if fmt == "e4m3":
        words = by_word.astype(ml_dtypes.float8_e4m3fn).view(np.uint8)
    else:
        c = by_word.astype(ml_dtypes.float4_e2m1fn).view(np.uint8) & 0xF
        words = (c[..., 0::2] | (c[..., 1::2] << 4)).reshape(k // 512, 128, 2 * n)
    return np.ascontiguousarray(words), np.ascontiguousarray(byte.astype(np.uint8).reshape(k // 512, 16, n))


def unpack_weight(words, scales, fmt):
    g, _, n = scales.shape
    words = np.ascontiguousarray(words).reshape(g, 128, n, -1)
    if fmt == "e4m3":
        vals = words.view(ml_dtypes.float8_e4m3fn).astype(np.float64)
    else:
        nib = np.empty((g, 128, n, 4), np.uint8)
        nib[..., 0::2] = words & 0xF
        nib[..., 1::2] = words >> 4
        vals = E2M1[nib]
    vals = vals * np.repeat(np.exp2(scales.astype(np.float64) - 127.0), 8, axis=1)[..., None]
    return vals.transpose(0, 1, 3, 2).reshape(g * 512, n)


K, J, R, T, U, F, O, N, E = 512, 512, 512, 1024, 1024, 1024, 256, 256, 128


def setup_inputs():
    n = np.random.standard_normal
    idx = np.stack([np.random.permutation(T)[:J] for _ in range(8)])
    idx2 = np.stack([np.random.permutation(U)[:J] for _ in range(8)])
    idx3 = np.stack([np.random.permutation(U)[:J] for _ in range(8)])
    idx4 = np.random.permutation(F)[:R]
    idx5 = np.stack([np.random.permutation(J)[:O] for _ in range(8)])
    idx6 = np.stack([np.random.permutation(O)[:E] for _ in range(8)])
    idx7 = np.stack([np.random.permutation(O)[:E] for _ in range(8)])
    fk = mx_kscale(K)
    fr = mx_kscale(R)
    tr = np.ones(F)
    tr[idx4] = fr
    wtp = pack_weight(n((K, F)) * 1 / np.sqrt(K) / fk[:, None] * tr, "e2m1")
    wbp = pack_weight(n((R, N)) * 1 / np.sqrt(R) / fr[:, None], "e4m3")
    wop = pack_weight(n((R, N)) * 1 / np.sqrt(R) / fr[:, None], "e2m1")
    return {
        "ta": (np.random.randint(-7, 8, (K, T)).astype(np.float64)).astype(np.float32),
        "ga": ((np.random.randint(8, 25, (K, 1)) / 64.0) * fk[:, None]).astype(np.float32),
        "gb": (np.random.uniform(0.5, 1.6, (K, 1))).astype(np.float32),
        "wt_words": wtp[0],
        "wt_scales": wtp[1],
        "sa": (np.random.uniform(0.5, 1.6, (R, 1))).astype(np.float32),
        "wb_words": wbp[0],
        "wb_scales": wbp[1],
        "wo_words": wop[0],
        "wo_scales": wop[1],
        "so": (np.random.uniform(0.5, 1.6, (N, 1))).astype(np.float32),
        "sp": (np.random.uniform(0.5, 1.6, (N, 1))).astype(np.float32),
        "offs": striped8(idx),
        "offs2": striped8(idx2),
        "offs3": striped8(idx3),
        "offs4": striped(idx4),
        "offs5": striped8(idx5),
        "offs6": striped8(idx6),
        "offs7": striped8(idx7),
    }


def reference(ta, ga, gb, wt_words, wt_scales, sa, wb_words, wb_scales, wo_words, wo_scales, so, sp, offs, offs2, offs3, offs4, offs5, offs6, offs7):
    idx = unstriped8(offs)
    idx2 = unstriped8(offs2)
    idx3 = unstriped8(offs3)
    idx4 = unstriped(offs4)
    idx5 = unstriped8(offs5)
    idx6 = unstriped8(offs6)
    idx7 = unstriped8(offs7)
    wtu = unpack_weight(wt_words, wt_scales, "e2m1")
    wbu = unpack_weight(wb_words, wb_scales, "e4m3")
    wou = unpack_weight(wo_words, wo_scales, "e2m1")
    xcd = pick8(f64(ta), idx, 64) * f64(ga)
    xcp = np.zeros((K, U))
    xcp[np.arange(K)[:, None], idx2[np.arange(K) % 512 // 64]] = xcd
    xc = pick8(xcp, idx3, 64) * f64(gb)
    wtidx4g = wtu[:, idx4]
    xcq = mxq(xc, 0, "e4m3")
    a = wtidx4g.T @ xcq
    g1 = np.maximum(a, 0.0)
    hid = pick8(g1, idx5, 64) * f64(sa)
    hidq = mxq(hid, 0, "e4m3")
    p = wbu.T @ hidq
    q = wou.T @ hidq
    y = pick8(p, idx6, 16) * f64(so) - pick8(q, idx7, 16) * f64(sp)
    return y

@@ -1,0 +1,242 @@
+from contextlib import ExitStack
+
+import concourse.mybir as mybir
+
+K, J, R, T, U, F, O, N, E = 512, 512, 512, 1024, 1024, 1024, 256, 256, 128
+FLOPS = 2 * K * R * J + 2 * 2 * R * N * O
+
+F32 = mybir.dt.float32
+BF16 = mybir.dt.bfloat16
+I32 = mybir.dt.int32
+U32 = mybir.dt.uint32
+U16 = mybir.dt.uint16
+U8 = mybir.dt.uint8
+FP8X4 = mybir.dt.float8_e4m3fn_x4
+FP4X4 = mybir.dt.float4_e2m1fn_x4
+COPY = mybir.ActivationFunctionType.Copy
+RELU = mybir.ActivationFunctionType.Relu
+
+P = 128
+PACK = 4
+LANE = 16
+ALIGN = 64
+
+
+def entries(offsets, first, count):
+    return offsets[:, first // LANE : (first + count) // LANE]
+
+
+def load_scale_rows(nc, plane, scales):
+    for quad in range(4):
+        nc.sync.dma_start(
+            out=plane[32 * quad : 32 * quad + 4, :].bitcast(I32),
+            in_=scales[0, 4 * quad : 4 * quad + 4, :].bitcast(I32),
+        )
+
+
+def weave_pair(copy, woven, planes, first):
+    copy(woven[:, :, first : first + 2], planes[:, first : first + 2, :].rearrange("p t j -> p j t"))
+
+
+def interleave(nc, woven, planes):
+    nc.vector.tensor_copy(
+        out=woven[:].rearrange("p (c i) t -> p c t i", i=4),
+        in_=planes[:].rearrange("p t (c i) -> p c t i", i=4),
+    )
+
+
+def tile_picked_codepage_store_one_kept_outcomes_outmeet_kernel(
+    tc, ta, ga, gb, wt_words, wt_scales, sa, wb_words, wb_scales, wo_words, wo_scales, so, sp,
+    offs, offs2, offs3, offs4, offs5, offs6, offs7, out,
+):
+    nc = tc.nc
+    JH = J // 2
+    OH = O // 2
+
+    with ExitStack() as ctx:
+        lists = ctx.enter_context(tc.tile_pool(name="lists", bufs=1))
+        keep = ctx.enter_context(tc.tile_pool(name="keep", bufs=1))
+        over = ctx.enter_context(tc.tile_pool(name="over", bufs=1))
+        psum = ctx.enter_context(tc.psum_pool(name="psum", bufs=1))
+
+        def load_list(source, name):
+            tile = lists.tile(list(source.shape), U16, name=name)
+            nc.sync.dma_start(tile[:], source)
+            return tile
+
+        def load_column(source, name):
+            tile = keep.tile([P, PACK], F32, name=name)
+            nc.sync.dma_start(out=tile[:], in_=source.rearrange("(p t) o -> p (t o)", t=PACK))
+            return tile
+
+        wts_win = keep.tile([P, F], U8, name="wts_win")
+        for first, last in ((0, 16), (32, 64), (64, 128)):
+            nc.vector.memset(wts_win[first:last, :].bitcast(I32), 0)
+        wt_sc = keep.tile([P, R], U8, name="wt_sc", align_bytes=ALIGN)
+        out_scales = keep.tile([P, 2 * N], U8, name="out_scales", align_bytes=ALIGN)
+        pages = [keep.tile([P, U], F32, name="page%d" % i) for i in range(2)]
+        nc.vector.memset(pages[0][:], 0.0)
+        nc.vector.memset(out_scales[:].bitcast(I32), 0)
+        nc.vector.memset(wt_sc[:].bitcast(I32), 0)
+        nc.vector.memset(pages[1][:], 0.0)
+
+        zero = keep.tile([P, 1], F32, name="zero", tag="hid1", align_bytes=ALIGN)
+        nc.vector.memset(zero[:], 0.0)
+
+        ta_rows = ta.rearrange("(p t) c -> t p c", t=PACK)
+        ta_sb = [keep.tile([P, T], F32, name="ta%d" % t) for t in range(PACK - 1)]
+        ta_sb.append(over.tile([P, T], F32, name="ta3", offset=0, align_bytes=ALIGN))
+
+        l1 = load_list(offs, "l1")
+        ga_sb = load_column(ga, "ga_sb")
+        l4 = load_list(offs4, "l4")
+        nc.sync.dma_start(out=wts_win[16:32, :].bitcast(I32), in_=wt_scales[0].bitcast(I32))
+        wtw_win = keep.tile([P, F], U16, name="wtw_win")
+        nc.sync.dma_start(out=wtw_win[:].bitcast(I32), in_=wt_words[0].bitcast(I32))
+        nc.sync.dma_start(out=ta_sb[0][:], in_=ta_rows[0])
+        l2 = load_list(offs2, "l2")
+        for t in range(1, PACK):
+            nc.sync.dma_start(out=ta_sb[t][:], in_=ta_rows[t])
+        l3 = load_list(offs3, "l3")
+        gb_sb = load_column(gb, "gb_sb")
+        l5 = load_list(offs5, "l5")
+        sa_sb = load_column(sa, "sa_sb")
+        wb_sb = keep.tile([P, N], U32, name="wb_sb", align_bytes=ALIGN)
+        nc.sync.dma_start(out=wb_sb[:].bitcast(I32), in_=wb_words[0].rearrange("p n t -> p (n t)").bitcast(I32))
+        wo_sb = keep.tile([P, 2 * N], U8, name="wo_sb", align_bytes=ALIGN)
+        nc.sync.dma_start(out=wo_sb[:].bitcast(I32), in_=wo_words[0].bitcast(I32))
+        load_scale_rows(nc, out_scales[:, 0:N], wb_scales)
+        load_scale_rows(nc, out_scales[:, N : 2 * N], wo_scales)
+        l6 = load_list(offs6, "l6")
+        l7 = load_list(offs7, "l7")
+        so_sb = keep.tile([P, 2, 1], F32, name="so_sb")
+        sp_sb = keep.tile([P, 2, 1], F32, name="sp_sb")
+        with nc.allow_non_contiguous_dma(reason="one weight a partition and block of output rows"):
+            nc.sync.dma_start(out=so_sb[:], in_=so.rearrange("(u p) o -> p u o", p=P))
+            nc.sync.dma_start(out=sp_sb[:], in_=sp.rearrange("(u p) o -> p u o", p=P))
+
+        sc_picked = keep.tile([P, R], U8, name="sc_picked")
+        nc.vector.tensor_copy(sc_picked[:].rearrange("p (t m) -> p m t", t=PACK), wts_win[:].indirect(l4[:]))
+        wt_picked = keep.tile([P, R], U16, name="wt_picked")
+        nc.vector.tensor_copy(wt_picked[:], wtw_win[:].indirect(l4[:]))
+        for quad in range(4):
+            nc.sync.dma_start(
+                out=wt_sc[32 * quad : 32 * quad + 4, :].bitcast(I32),
+                in_=sc_picked[16 + 4 * quad : 16 + 4 * quad + 4, :].bitcast(I32),
+            )
+
+        xcd = [keep.tile([P, J], F32, name="xcd%d" % t, tag="xcd%d" % t, align_bytes=ALIGN) for t in range(PACK)]
+        for t in range(PACK):
+            pieces = 2 if t == 0 else 1
+            size = J // pieces
+            for h in range(pieces):
+                nc.scalar.activation(
+                    out=xcd[t][:, h * size : (h + 1) * size],
+                    in_=ta_sb[t][:].indirect(entries(l1, h * size, size)),
+                    func=COPY,
+                    scale=ga_sb[:, t : t + 1],
+                )
+
+        xc_planes = [
+            over.tile([P, PACK, JH], BF16, name="xc_planes%d" % h, offset=h * PACK * JH * 2, align_bytes=ALIGN)
+            for h in range(2)
+        ]
+        xc_woven = [keep.tile([P, JH, PACK], BF16, name="xc_woven%d" % h, align_bytes=ALIGN) for h in range(2)]
+        for t in range(PACK):
+            page = pages[t % 2]
+            pieces = 2 if t == 0 else 1
+            size = J // pieces
+            for h in range(pieces):
+                nc.vector.tensor_copy(
+                    page[:].indirect(entries(l2, h * size, size)), xcd[t][:, h * size : (h + 1) * size]
+                )
+            for h in range(2):
+                nc.scalar.activation(
+                    out=xc_planes[h][:, t, :],
+                    in_=page[:].indirect(entries(l3, h * JH, JH)),
+                    func=COPY,
+                    scale=gb_sb[:, t : t + 1],
+                )
+            if t == 1:
+                for h in range(2):
+                    weave_pair(nc.scalar.copy, xc_woven[h], xc_planes[h], 0)
+
+        wt_dealt = keep.tile([P, 2 * R], U8, name="wt_dealt", tag="xcd%d" % (PACK - 1), align_bytes=ALIGN)
+        nc.vector.tensor_copy(
+            out=wt_dealt[:].rearrange("p (t c i b) -> p c t i b", t=PACK, i=8, b=2),
+            in_=wt_picked[:].bitcast(U8).rearrange("p (c i t b) -> p c t i b", t=PACK, i=8, b=2),
+        )
+
+        g1 = [keep.tile([P, J], F32, name="g1_%d" % t) for t in range(PACK)]
+        for h in range(2):
+            weave_pair(nc.vector.tensor_copy, xc_woven[h], xc_planes[h], 2)
+            xc_codes = keep.tile([P, JH], U32, name="xc_codes%d" % h, align_bytes=ALIGN)
+            xc_scales = keep.tile([P, JH], U8, name="xc_scales%d" % h, align_bytes=ALIGN)
+            nc.vector.quantize_mx(
+                out=xc_codes[:].bitcast(FP8X4), scales=xc_scales[:], in_=xc_woven[h][:].rearrange("p j t -> p (j t)")
+            )
+            for t in range(PACK):
+                acc = psum.tile([P, JH], F32, name="a%d_%d" % (h, t), tag="bank%d" % (PACK * h + t))
+                nc.tensor.matmul_mx(
+                    out=acc[:],
+                    lhsT=wt_dealt[:, 2 * P * t : 2 * P * (t + 1)].bitcast(FP4X4),
+                    lhsT_scale=wt_sc[:, P * t : P * (t + 1)],
+                    rhs=xc_codes[:].bitcast(FP8X4),
+                    rhs_scale=xc_scales[:],
+                    start=True,
+                    stop=True,
+                )
+                if h == 0:
+                    nc.scalar.activation(out=g1[t][:, 0:JH], in_=acc[:], func=RELU)
+                else:
+                    nc.vector.tensor_scalar_max(g1[t][:, JH:J], acc[:], zero[:])
+
+        results = [keep.tile([P, O], F32, name="result%d" % i) for i in range(4)]
+        for h in range(2):
+            hid_planes = keep.tile([P, PACK, OH], BF16, name="hid_planes%d" % h, tag="hid%d" % h, align_bytes=ALIGN)
+            for t in range(PACK):
+                nc.scalar.activation(
+                    out=hid_planes[:, t, :],
+                    in_=g1[t][:].indirect(entries(l5, h * OH, OH)),
+                    func=COPY,
+                    scale=sa_sb[:, t : t + 1],
+                )
+            hid_woven = keep.tile([P, OH, PACK], BF16, name="hid_woven%d" % h, align_bytes=ALIGN)
+            interleave(nc, hid_woven, hid_planes)
+            hid_codes = keep.tile([P, OH], U32, name="hid_codes%d" % h, align_bytes=ALIGN)
+            hid_scales = keep.tile([P, OH], U8, name="hid_scales%d" % h, align_bytes=ALIGN)
+            nc.vector.quantize_mx(
+                out=hid_codes[:].bitcast(FP8X4), scales=hid_scales[:], in_=hid_woven[:].rearrange("p j t -> p (j t)")
+            )
+            for u in range(2):
+                for second in range(2):
+                    i = 2 * u + second
+                    if second:
+                        weights = wo_sb[:, 2 * P * u : 2 * P * (u + 1)].bitcast(FP4X4)
+                    else:
+                        weights = wb_sb[:, P * u : P * (u + 1)].bitcast(FP8X4)
+                    acc = psum.tile([P, OH], F32, name="r%d_%d" % (h, i), tag="bank%d" % (PACK * h + i))
+                    nc.tensor.matmul_mx(
+                        out=acc[:],
+                        lhsT=weights,
+                        lhsT_scale=out_scales[:, N * second + P * u : N * second + P * (u + 1)],
+                        rhs=hid_codes[:].bitcast(FP8X4),
+                        rhs_scale=hid_scales[:],
+                        start=True,
+                        stop=True,
+                    )
+                    if h == 0:
+                        nc.scalar.copy(results[i][:, 0:OH], acc[:])
+                    else:
+                        nc.vector.tensor_copy(results[i][:, OH:O], acc[:])
+
+        for u in range(2):
+            first = keep.tile([P, E], F32, name="first%d" % u)
+            nc.scalar.activation(out=first[:], in_=results[2 * u][:].indirect(l6[:]), func=COPY, scale=so_sb[:, u, :])
+            second = keep.tile([P, E], F32, name="second%d" % u)
+            nc.scalar.activation(
+                out=second[:], in_=results[2 * u + 1][:].indirect(l7[:]), func=COPY, scale=sp_sb[:, u, :]
+            )
+            met = keep.tile([P, E], F32, name="met%d" % u)
+            nc.vector.tensor_sub(met[:], first[:], second[:])
+            nc.sync.dma_start(out=out[P * u : P * (u + 1), :], in_=met[:])

@@ -69,6 +69,10 @@ def tile_picked_codepage_store_one_kept_outcomes_outmeet_kernel(
             nc.sync.dma_start(out=tile[:], in_=source.rearrange("(p t) o -> p (t o)", t=PACK))
             return tile
 
+        warm_in = keep.tile([P, 1], F32, name="warm_in")
+        warm_out = keep.tile([P, 1], F32, name="warm_out")
+        nc.gpsimd.memset(warm_in[:], 0.0)
+        nc.scalar.activation(out=warm_out[:], in_=warm_in[:], func=COPY)
         wts_win = keep.tile([P, F], U8, name="wts_win")
         for first, last in ((0, 16), (32, 64), (64, 128)):
             nc.vector.memset(wts_win[first:last, :].bitcast(I32), 0)

@@ -35,14 +35,7 @@ def load_scale_rows(nc, plane, scales):
 
 
 def weave_pair(copy, woven, planes, first):
-    copy(woven[:, :, first : first + 2], planes[:, first : first + 2, :].rearrange("p t j -> p j t"))
-
-
-def interleave(nc, woven, planes):
-    nc.vector.tensor_copy(
-        out=woven[:].rearrange("p (c i) t -> p c t i", i=4),
-        in_=planes[:].rearrange("p t (c i) -> p c t i", i=4),
-    )
+    copy(woven[:, :, first : first + 2], planes.rearrange("p t j -> p j t"))
 
 
 def tile_picked_codepage_store_one_kept_outcomes_outmeet_kernel(
@@ -64,9 +57,9 @@ def tile_picked_codepage_store_one_kept_outcomes_outmeet_kernel(
             nc.sync.dma_start(tile[:], source)
             return tile
 
-        def load_column(source, name):
+        def load_column(queue, source, name):
             tile = keep.tile([P, PACK], F32, name=name)
-            nc.sync.dma_start(out=tile[:], in_=source.rearrange("(p t) o -> p (t o)", t=PACK))
+            queue.dma_start(out=tile[:], in_=source.rearrange("(p t) o -> p (t o)", t=PACK))
             return tile
 
         warm_in = keep.tile([P, 1], F32, name="warm_in")
@@ -80,31 +73,31 @@ def tile_picked_codepage_store_one_kept_outcomes_outmeet_kernel(
         out_scales = keep.tile([P, 2 * N], U8, name="out_scales", align_bytes=ALIGN)
         pages = [keep.tile([P, U], F32, name="page%d" % i) for i in range(2)]
         nc.vector.memset(pages[0][:], 0.0)
-        nc.vector.memset(out_scales[:].bitcast(I32), 0)
-        nc.vector.memset(wt_sc[:].bitcast(I32), 0)
-        nc.vector.memset(pages[1][:], 0.0)
+        nc.gpsimd.memset(pages[1][:], 0.0)
+        nc.gpsimd.memset(out_scales[:].bitcast(I32), 0)
+        nc.gpsimd.memset(wt_sc[:].bitcast(I32), 0)
 
-        zero = keep.tile([P, 1], F32, name="zero", tag="hid1", align_bytes=ALIGN)
-        nc.vector.memset(zero[:], 0.0)
+        zero = keep.tile([P, 1], F32, name="zero", tag="zero", align_bytes=ALIGN)
+        nc.gpsimd.memset(zero[:], 0.0)
 
         ta_rows = ta.rearrange("(p t) c -> t p c", t=PACK)
         ta_sb = [keep.tile([P, T], F32, name="ta%d" % t) for t in range(PACK - 1)]
         ta_sb.append(over.tile([P, T], F32, name="ta3", offset=0, align_bytes=ALIGN))
 
-        l1 = load_list(offs, "l1")
-        ga_sb = load_column(ga, "ga_sb")
+        ga_sb = load_column(nc.scalar, ga, "ga_sb")
         l4 = load_list(offs4, "l4")
         nc.sync.dma_start(out=wts_win[16:32, :].bitcast(I32), in_=wt_scales[0].bitcast(I32))
         wtw_win = keep.tile([P, F], U16, name="wtw_win")
         nc.sync.dma_start(out=wtw_win[:].bitcast(I32), in_=wt_words[0].bitcast(I32))
+        l1 = load_list(offs, "l1")
         nc.sync.dma_start(out=ta_sb[0][:], in_=ta_rows[0])
         l2 = load_list(offs2, "l2")
         for t in range(1, PACK):
             nc.sync.dma_start(out=ta_sb[t][:], in_=ta_rows[t])
         l3 = load_list(offs3, "l3")
-        gb_sb = load_column(gb, "gb_sb")
+        gb_sb = load_column(nc.sync, gb, "gb_sb")
         l5 = load_list(offs5, "l5")
-        sa_sb = load_column(sa, "sa_sb")
+        sa_sb = load_column(nc.sync, sa, "sa_sb")
         wb_sb = keep.tile([P, N], U32, name="wb_sb", align_bytes=ALIGN)
         nc.sync.dma_start(out=wb_sb[:].bitcast(I32), in_=wb_words[0].rearrange("p n t -> p (n t)").bitcast(I32))
         wo_sb = keep.tile([P, 2 * N], U8, name="wo_sb", align_bytes=ALIGN)
@@ -163,7 +156,7 @@ def tile_picked_codepage_store_one_kept_outcomes_outmeet_kernel(
                 )
             if t == 1:
                 for h in range(2):
-                    weave_pair(nc.scalar.copy, xc_woven[h], xc_planes[h], 0)
+                    weave_pair(nc.scalar.copy, xc_woven[h][:], xc_planes[h][:, 0:2, :], 0)
 
         wt_dealt = keep.tile([P, 2 * R], U8, name="wt_dealt", tag="xcd%d" % (PACK - 1), align_bytes=ALIGN)
         nc.vector.tensor_copy(
@@ -171,68 +164,88 @@ def tile_picked_codepage_store_one_kept_outcomes_outmeet_kernel(
             in_=wt_picked[:].bitcast(U8).rearrange("p (c i t b) -> p c t i b", t=PACK, i=8, b=2),
         )
 
-        g1 = [keep.tile([P, J], F32, name="g1_%d" % t) for t in range(PACK)]
+        xc_codes = keep.tile([P, J], U32, name="xc_codes", align_bytes=ALIGN)
+        xc_scales = keep.tile([P, J], U8, name="xc_scales", align_bytes=ALIGN)
         for h in range(2):
-            weave_pair(nc.vector.tensor_copy, xc_woven[h], xc_planes[h], 2)
-            xc_codes = keep.tile([P, JH], U32, name="xc_codes%d" % h, align_bytes=ALIGN)
-            xc_scales = keep.tile([P, JH], U8, name="xc_scales%d" % h, align_bytes=ALIGN)
+            weave_pair(nc.vector.tensor_copy, xc_woven[h][:], xc_planes[h][:, 2:4, :], 2)
+        for h in range(2):
             nc.vector.quantize_mx(
-                out=xc_codes[:].bitcast(FP8X4), scales=xc_scales[:], in_=xc_woven[h][:].rearrange("p j t -> p (j t)")
+                out=xc_codes[:, h * JH : (h + 1) * JH].bitcast(FP8X4),
+                scales=xc_scales[:, h * JH : (h + 1) * JH],
+                in_=xc_woven[h][:].rearrange("p j t -> p (j t)"),
             )
-            for t in range(PACK):
-                acc = psum.tile([P, JH], F32, name="a%d_%d" % (h, t), tag="bank%d" % (PACK * h + t))
-                nc.tensor.matmul_mx(
-                    out=acc[:],
-                    lhsT=wt_dealt[:, 2 * P * t : 2 * P * (t + 1)].bitcast(FP4X4),
-                    lhsT_scale=wt_sc[:, P * t : P * (t + 1)],
-                    rhs=xc_codes[:].bitcast(FP8X4),
-                    rhs_scale=xc_scales[:],
-                    start=True,
-                    stop=True,
-                )
-                if h == 0:
-                    nc.scalar.activation(out=g1[t][:, 0:JH], in_=acc[:], func=RELU)
-                else:
-                    nc.vector.tensor_scalar_max(g1[t][:, JH:J], acc[:], zero[:])
+
+        banks = [i % 8 for i in range(10)]
+
+        def product(name, weights, weight_scales, codes, scales, first, last):
+            acc = psum.tile([P, last - first], F32, name=name, tag="bank%d" % banks.pop(0))
+            nc.tensor.matmul_mx(
+                out=acc[:],
+                lhsT=weights,
+                lhsT_scale=weight_scales,
+                rhs=codes[:, first:last].bitcast(FP8X4),
+                rhs_scale=scales[:, first:last],
+                start=True,
+                stop=True,
+            )
+            return acc
+
+        g1 = [keep.tile([P, J], F32, name="g1_%d" % t) for t in range(PACK)]
+        for t in range(PACK):
+            weights = wt_dealt[:, 2 * P * t : 2 * P * (t + 1)].bitcast(FP4X4)
+            weight_scales = wt_sc[:, P * t : P * (t + 1)]
+            if t == 0:
+                acc = product("a0_low", weights, weight_scales, xc_codes, xc_scales, 0, JH)
+                nc.scalar.activation(out=g1[t][:, 0:JH], in_=acc[:], func=RELU)
+                acc = product("a0_high", weights, weight_scales, xc_codes, xc_scales, JH, J)
+                nc.vector.tensor_scalar_max(g1[t][:, JH:J], acc[:], zero[:])
+            else:
+                acc = product("a%d" % t, weights, weight_scales, xc_codes, xc_scales, 0, J)
+                nc.vector.tensor_scalar_max(g1[t][:], acc[:], zero[:])
+
+        def fetch_hidden(plane, t, first, count):
+            nc.scalar.activation(
+                out=plane, in_=g1[t][:].indirect(entries(l5, first, count)), func=COPY, scale=sa_sb[:, t : t + 1]
+            )
+
+        hid_early = keep.tile([P, 2, O], BF16, name="hid_early")
+        for t in range(2):
+            fetch_hidden(hid_early[:, t, :], t, 0, O)
+        hid_late = [keep.tile([P, 2, OH], BF16, name="hid_late%d" % h) for h in range(2)]
+        for t in range(2, PACK):
+            for h in range(2):
+                fetch_hidden(hid_late[h][:, t - 2, :], t, h * OH, OH)
+
+        hid_woven = keep.tile([P, O, PACK], BF16, name="hid_woven", tag="zero", align_bytes=ALIGN)
+        weave_pair(nc.vector.tensor_copy, hid_woven[:], hid_early[:], 0)
+        hid_codes = keep.tile([P, O], U32, name="hid_codes", align_bytes=ALIGN)
+        hid_scales = keep.tile([P, O], U8, name="hid_scales", align_bytes=ALIGN)
+        for h in range(2):
+            weave_pair(nc.vector.tensor_copy, hid_woven[:, h * OH : (h + 1) * OH, :], hid_late[h][:], 2)
+        for h in range(2):
+            nc.vector.quantize_mx(
+                out=hid_codes[:, h * OH : (h + 1) * OH].bitcast(FP8X4),
+                scales=hid_scales[:, h * OH : (h + 1) * OH],
+                in_=hid_woven[:, h * OH : (h + 1) * OH, :].rearrange("p o t -> p (o t)"),
+            )
 
         results = [keep.tile([P, O], F32, name="result%d" % i) for i in range(4)]
-        for h in range(2):
-            hid_planes = keep.tile([P, PACK, OH], BF16, name="hid_planes%d" % h, tag="hid%d" % h, align_bytes=ALIGN)
-            for t in range(PACK):
-                nc.scalar.activation(
-                    out=hid_planes[:, t, :],
-                    in_=g1[t][:].indirect(entries(l5, h * OH, OH)),
-                    func=COPY,
-                    scale=sa_sb[:, t : t + 1],
-                )
-            hid_woven = keep.tile([P, OH, PACK], BF16, name="hid_woven%d" % h, align_bytes=ALIGN)
-            interleave(nc, hid_woven, hid_planes)
-            hid_codes = keep.tile([P, OH], U32, name="hid_codes%d" % h, align_bytes=ALIGN)
-            hid_scales = keep.tile([P, OH], U8, name="hid_scales%d" % h, align_bytes=ALIGN)
-            nc.vector.quantize_mx(
-                out=hid_codes[:].bitcast(FP8X4), scales=hid_scales[:], in_=hid_woven[:].rearrange("p j t -> p (j t)")
-            )
-            for u in range(2):
-                for second in range(2):
-                    i = 2 * u + second
-                    if second:
-                        weights = wo_sb[:, 2 * P * u : 2 * P * (u + 1)].bitcast(FP4X4)
-                    else:
-                        weights = wb_sb[:, P * u : P * (u + 1)].bitcast(FP8X4)
-                    acc = psum.tile([P, OH], F32, name="r%d_%d" % (h, i), tag="bank%d" % (PACK * h + i))
-                    nc.tensor.matmul_mx(
-                        out=acc[:],
-                        lhsT=weights,
-                        lhsT_scale=out_scales[:, N * second + P * u : N * second + P * (u + 1)],
-                        rhs=hid_codes[:].bitcast(FP8X4),
-                        rhs_scale=hid_scales[:],
-                        start=True,
-                        stop=True,
-                    )
-                    if h == 0:
-                        nc.scalar.copy(results[i][:, 0:OH], acc[:])
-                    else:
-                        nc.vector.tensor_copy(results[i][:, OH:O], acc[:])
+        for u in range(2):
+            for second in range(2):
+                i = 2 * u + second
+                if second:
+                    weights = wo_sb[:, 2 * P * u : 2 * P * (u + 1)].bitcast(FP4X4)
+                else:
+                    weights = wb_sb[:, P * u : P * (u + 1)].bitcast(FP8X4)
+                weight_scales = out_scales[:, N * second + P * u : N * second + P * (u + 1)]
+                if i == 0:
+                    acc = product("r0_low", weights, weight_scales, hid_codes, hid_scales, 0, OH)
+                    nc.scalar.copy(results[i][:, 0:OH], acc[:])
+                    acc = product("r0_high", weights, weight_scales, hid_codes, hid_scales, OH, O)
+                    nc.vector.tensor_copy(results[i][:, OH:O], acc[:])
+                else:
+                    acc = product("r%d" % i, weights, weight_scales, hid_codes, hid_scales, 0, O)
+                    nc.vector.tensor_copy(results[i][:], acc[:])
 
         for u in range(2):
             first = keep.tile([P, E], F32, name="first%d" % u)

@@ -84,13 +84,13 @@ def tile_picked_codepage_store_one_kept_outcomes_outmeet_kernel(
         ta_sb = [keep.tile([P, T], F32, name="ta%d" % t) for t in range(PACK - 1)]
         ta_sb.append(over.tile([P, T], F32, name="ta3", offset=0, align_bytes=ALIGN))
 
+        wtw_win = keep.tile([P, F], U16, name="wtw_win")
+        nc.scalar.dma_start(out=wtw_win[:].bitcast(I32), in_=wt_words[0].bitcast(I32))
         ga_sb = load_column(nc.scalar, ga, "ga_sb")
         l4 = load_list(offs4, "l4")
         nc.sync.dma_start(out=wts_win[16:32, :].bitcast(I32), in_=wt_scales[0].bitcast(I32))
-        wtw_win = keep.tile([P, F], U16, name="wtw_win")
-        nc.sync.dma_start(out=wtw_win[:].bitcast(I32), in_=wt_words[0].bitcast(I32))
-        l1 = load_list(offs, "l1")
         nc.sync.dma_start(out=ta_sb[0][:], in_=ta_rows[0])
+        l1 = load_list(offs, "l1")
         l2 = load_list(offs2, "l2")
         for t in range(1, PACK):
             nc.sync.dma_start(out=ta_sb[t][:], in_=ta_rows[t])

@@ -81,8 +81,12 @@ def tile_picked_codepage_store_one_kept_outcomes_outmeet_kernel(
         nc.gpsimd.memset(zero[:], 0.0)
 
         ta_rows = ta.rearrange("(p t) c -> t p c", t=PACK)
-        ta_sb = [keep.tile([P, T], F32, name="ta%d" % t) for t in range(PACK - 1)]
-        ta_sb.append(over.tile([P, T], F32, name="ta3", offset=0, align_bytes=ALIGN))
+        ta_sb = [
+            over.tile([P, T], F32, name="ta2", offset=0, align_bytes=ALIGN)
+            if t == 2
+            else keep.tile([P, T], F32, name="ta%d" % t)
+            for t in range(PACK)
+        ]
 
         wtw_win = keep.tile([P, F], U16, name="wtw_win")
         nc.scalar.dma_start(out=wtw_win[:].bitcast(I32), in_=wt_words[0].bitcast(I32))

from contextlib import ExitStack

import concourse.mybir as mybir

K, J, R, T, U, F, O, N, E = 512, 512, 512, 1024, 1024, 1024, 256, 256, 128
FLOPS = 2 * K * R * J + 2 * 2 * R * N * O

F32 = mybir.dt.float32
BF16 = mybir.dt.bfloat16
I32 = mybir.dt.int32
U32 = mybir.dt.uint32
U16 = mybir.dt.uint16
U8 = mybir.dt.uint8
FP8X4 = mybir.dt.float8_e4m3fn_x4
FP4X4 = mybir.dt.float4_e2m1fn_x4
COPY = mybir.ActivationFunctionType.Copy
RELU = mybir.ActivationFunctionType.Relu

P = 128
PACK = 4
LANE = 16
ALIGN = 64


def entries(offsets, first, count):
    return offsets[:, first // LANE : (first + count) // LANE]


def load_scale_rows(nc, plane, scales):
    for quad in range(4):
        nc.sync.dma_start(
            out=plane[32 * quad : 32 * quad + 4, :].bitcast(I32),
            in_=scales[0, 4 * quad : 4 * quad + 4, :].bitcast(I32),
        )


def weave_pair(copy, woven, planes, first):
    copy(woven[:, :, first : first + 2], planes.rearrange("p t j -> p j t"))


def tile_picked_codepage_store_one_kept_outcomes_outmeet_kernel(
    tc, ta, ga, gb, wt_words, wt_scales, sa, wb_words, wb_scales, wo_words, wo_scales, so, sp,
    offs, offs2, offs3, offs4, offs5, offs6, offs7, out,
):
    nc = tc.nc
    JH = J // 2
    OH = O // 2

    with ExitStack() as ctx:
        lists = ctx.enter_context(tc.tile_pool(name="lists", bufs=1))
        keep = ctx.enter_context(tc.tile_pool(name="keep", bufs=1))
        over = ctx.enter_context(tc.tile_pool(name="over", bufs=1))
        psum = ctx.enter_context(tc.psum_pool(name="psum", bufs=1))

        def load_list(source, name):
            tile = lists.tile(list(source.shape), U16, name=name)
            nc.sync.dma_start(tile[:], source)
            return tile

        def load_column(queue, source, name):
            tile = keep.tile([P, PACK], F32, name=name)
            queue.dma_start(out=tile[:], in_=source.rearrange("(p t) o -> p (t o)", t=PACK))
            return tile

        warm_in = keep.tile([P, 1], F32, name="warm_in")
        warm_out = keep.tile([P, 1], F32, name="warm_out")
        nc.gpsimd.memset(warm_in[:], 0.0)
        nc.scalar.activation(out=warm_out[:], in_=warm_in[:], func=COPY)
        wts_win = keep.tile([P, F], U8, name="wts_win")
        for first, last in ((0, 16), (32, 64), (64, 128)):
            nc.vector.memset(wts_win[first:last, :].bitcast(I32), 0)
        wt_sc = keep.tile([P, R], U8, name="wt_sc", align_bytes=ALIGN)
        out_scales = keep.tile([P, 2 * N], U8, name="out_scales", align_bytes=ALIGN)
        pages = [keep.tile([P, U], F32, name="page%d" % i) for i in range(2)]
        nc.vector.memset(pages[0][:], 0.0)
        nc.gpsimd.memset(pages[1][:], 0.0)
        nc.gpsimd.memset(out_scales[:].bitcast(I32), 0)
        nc.gpsimd.memset(wt_sc[:].bitcast(I32), 0)

        zero = keep.tile([P, 1], F32, name="zero", tag="zero", align_bytes=ALIGN)
        nc.gpsimd.memset(zero[:], 0.0)

        ta_rows = ta.rearrange("(p t) c -> t p c", t=PACK)
        ta_sb = [
            over.tile([P, T], F32, name="ta2", offset=0, align_bytes=ALIGN)
            if t == 2
            else keep.tile([P, T], F32, name="ta%d" % t)
            for t in range(PACK)
        ]

        wtw_win = keep.tile([P, F], U16, name="wtw_win")
        nc.scalar.dma_start(out=wtw_win[:].bitcast(I32), in_=wt_words[0].bitcast(I32))
        ga_sb = load_column(nc.scalar, ga, "ga_sb")
        l4 = load_list(offs4, "l4")
        nc.sync.dma_start(out=wts_win[16:32, :].bitcast(I32), in_=wt_scales[0].bitcast(I32))
        nc.sync.dma_start(out=ta_sb[0][:], in_=ta_rows[0])
        l1 = load_list(offs, "l1")
        l2 = load_list(offs2, "l2")
        for t in range(1, PACK):
            nc.sync.dma_start(out=ta_sb[t][:], in_=ta_rows[t])
        l3 = load_list(offs3, "l3")
        gb_sb = load_column(nc.sync, gb, "gb_sb")
        l5 = load_list(offs5, "l5")
        sa_sb = load_column(nc.sync, sa, "sa_sb")
        wb_sb = keep.tile([P, N], U32, name="wb_sb", align_bytes=ALIGN)
        nc.sync.dma_start(out=wb_sb[:].bitcast(I32), in_=wb_words[0].rearrange("p n t -> p (n t)").bitcast(I32))
        wo_sb = keep.tile([P, 2 * N], U8, name="wo_sb", align_bytes=ALIGN)
        nc.sync.dma_start(out=wo_sb[:].bitcast(I32), in_=wo_words[0].bitcast(I32))
        load_scale_rows(nc, out_scales[:, 0:N], wb_scales)
        load_scale_rows(nc, out_scales[:, N : 2 * N], wo_scales)
        l6 = load_list(offs6, "l6")
        l7 = load_list(offs7, "l7")
        so_sb = keep.tile([P, 2, 1], F32, name="so_sb")
        sp_sb = keep.tile([P, 2, 1], F32, name="sp_sb")
        with nc.allow_non_contiguous_dma(reason="one weight a partition and block of output rows"):
            nc.sync.dma_start(out=so_sb[:], in_=so.rearrange("(u p) o -> p u o", p=P))
            nc.sync.dma_start(out=sp_sb[:], in_=sp.rearrange("(u p) o -> p u o", p=P))

        sc_picked = keep.tile([P, R], U8, name="sc_picked")
        nc.vector.tensor_copy(sc_picked[:].rearrange("p (t m) -> p m t", t=PACK), wts_win[:].indirect(l4[:]))
        wt_picked = keep.tile([P, R], U16, name="wt_picked")
        nc.vector.tensor_copy(wt_picked[:], wtw_win[:].indirect(l4[:]))
        for quad in range(4):
            nc.sync.dma_start(
                out=wt_sc[32 * quad : 32 * quad + 4, :].bitcast(I32),
                in_=sc_picked[16 + 4 * quad : 16 + 4 * quad + 4, :].bitcast(I32),
            )

        xcd = [keep.tile([P, J], F32, name="xcd%d" % t, tag="xcd%d" % t, align_bytes=ALIGN) for t in range(PACK)]
        for t in range(PACK):
            pieces = 2 if t == 0 else 1
            size = J // pieces
            for h in range(pieces):
                nc.scalar.activation(
                    out=xcd[t][:, h * size : (h + 1) * size],
                    in_=ta_sb[t][:].indirect(entries(l1, h * size, size)),
                    func=COPY,
                    scale=ga_sb[:, t : t + 1],
                )

        xc_planes = [
            over.tile([P, PACK, JH], BF16, name="xc_planes%d" % h, offset=h * PACK * JH * 2, align_bytes=ALIGN)
            for h in range(2)
        ]
        xc_woven = [keep.tile([P, JH, PACK], BF16, name="xc_woven%d" % h, align_bytes=ALIGN) for h in range(2)]
        for t in range(PACK):
            page = pages[t % 2]
            pieces = 2 if t == 0 else 1
            size = J // pieces
            for h in range(pieces):
                nc.vector.tensor_copy(
                    page[:].indirect(entries(l2, h * size, size)), xcd[t][:, h * size : (h + 1) * size]
                )
            for h in range(2):
                nc.scalar.activation(
                    out=xc_planes[h][:, t, :],
                    in_=page[:].indirect(entries(l3, h * JH, JH)),
                    func=COPY,
                    scale=gb_sb[:, t : t + 1],
                )
            if t == 1:
                for h in range(2):
                    weave_pair(nc.scalar.copy, xc_woven[h][:], xc_planes[h][:, 0:2, :], 0)

        wt_dealt = keep.tile([P, 2 * R], U8, name="wt_dealt", tag="xcd%d" % (PACK - 1), align_bytes=ALIGN)
        nc.vector.tensor_copy(
            out=wt_dealt[:].rearrange("p (t c i b) -> p c t i b", t=PACK, i=8, b=2),
            in_=wt_picked[:].bitcast(U8).rearrange("p (c i t b) -> p c t i b", t=PACK, i=8, b=2),
        )

        xc_codes = keep.tile([P, J], U32, name="xc_codes", align_bytes=ALIGN)
        xc_scales = keep.tile([P, J], U8, name="xc_scales", align_bytes=ALIGN)
        for h in range(2):
            weave_pair(nc.vector.tensor_copy, xc_woven[h][:], xc_planes[h][:, 2:4, :], 2)
        for h in range(2):
            nc.vector.quantize_mx(
                out=xc_codes[:, h * JH : (h + 1) * JH].bitcast(FP8X4),
                scales=xc_scales[:, h * JH : (h + 1) * JH],
                in_=xc_woven[h][:].rearrange("p j t -> p (j t)"),
            )

        banks = [i % 8 for i in range(10)]

        def product(name, weights, weight_scales, codes, scales, first, last):
            acc = psum.tile([P, last - first], F32, name=name, tag="bank%d" % banks.pop(0))
            nc.tensor.matmul_mx(
                out=acc[:],
                lhsT=weights,
                lhsT_scale=weight_scales,
                rhs=codes[:, first:last].bitcast(FP8X4),
                rhs_scale=scales[:, first:last],
                start=True,
                stop=True,
            )
            return acc

        g1 = [keep.tile([P, J], F32, name="g1_%d" % t) for t in range(PACK)]
        for t in range(PACK):
            weights = wt_dealt[:, 2 * P * t : 2 * P * (t + 1)].bitcast(FP4X4)
            weight_scales = wt_sc[:, P * t : P * (t + 1)]
            if t == 0:
                acc = product("a0_low", weights, weight_scales, xc_codes, xc_scales, 0, JH)
                nc.scalar.activation(out=g1[t][:, 0:JH], in_=acc[:], func=RELU)
                acc = product("a0_high", weights, weight_scales, xc_codes, xc_scales, JH, J)
                nc.vector.tensor_scalar_max(g1[t][:, JH:J], acc[:], zero[:])
            else:
                acc = product("a%d" % t, weights, weight_scales, xc_codes, xc_scales, 0, J)
                nc.vector.tensor_scalar_max(g1[t][:], acc[:], zero[:])

        def fetch_hidden(plane, t, first, count):
            nc.scalar.activation(
                out=plane, in_=g1[t][:].indirect(entries(l5, first, count)), func=COPY, scale=sa_sb[:, t : t + 1]
            )

        hid_early = keep.tile([P, 2, O], BF16, name="hid_early")
        for t in range(2):
            fetch_hidden(hid_early[:, t, :], t, 0, O)
        hid_late = [keep.tile([P, 2, OH], BF16, name="hid_late%d" % h) for h in range(2)]
        for t in range(2, PACK):
            for h in range(2):
                fetch_hidden(hid_late[h][:, t - 2, :], t, h * OH, OH)

        hid_woven = keep.tile([P, O, PACK], BF16, name="hid_woven", tag="zero", align_bytes=ALIGN)
        weave_pair(nc.vector.tensor_copy, hid_woven[:], hid_early[:], 0)
        hid_codes = keep.tile([P, O], U32, name="hid_codes", align_bytes=ALIGN)
        hid_scales = keep.tile([P, O], U8, name="hid_scales", align_bytes=ALIGN)
        for h in range(2):
            weave_pair(nc.vector.tensor_copy, hid_woven[:, h * OH : (h + 1) * OH, :], hid_late[h][:], 2)
        for h in range(2):
            nc.vector.quantize_mx(
                out=hid_codes[:, h * OH : (h + 1) * OH].bitcast(FP8X4),
                scales=hid_scales[:, h * OH : (h + 1) * OH],
                in_=hid_woven[:, h * OH : (h + 1) * OH, :].rearrange("p o t -> p (o t)"),
            )

        results = [keep.tile([P, O], F32, name="result%d" % i) for i in range(4)]
        for u in range(2):
            for second in range(2):
                i = 2 * u + second
                if second:
                    weights = wo_sb[:, 2 * P * u : 2 * P * (u + 1)].bitcast(FP4X4)
                else:
                    weights = wb_sb[:, P * u : P * (u + 1)].bitcast(FP8X4)
                weight_scales = out_scales[:, N * second + P * u : N * second + P * (u + 1)]
                if i == 0:
                    acc = product("r0_low", weights, weight_scales, hid_codes, hid_scales, 0, OH)
                    nc.scalar.copy(results[i][:, 0:OH], acc[:])
                    acc = product("r0_high", weights, weight_scales, hid_codes, hid_scales, OH, O)
                    nc.vector.tensor_copy(results[i][:, OH:O], acc[:])
                else:
                    acc = product("r%d" % i, weights, weight_scales, hid_codes, hid_scales, 0, O)
                    nc.vector.tensor_copy(results[i][:], acc[:])

        for u in range(2):
            first = keep.tile([P, E], F32, name="first%d" % u)
            nc.scalar.activation(out=first[:], in_=results[2 * u][:].indirect(l6[:]), func=COPY, scale=so_sb[:, u, :])
            second = keep.tile([P, E], F32, name="second%d" % u)
            nc.scalar.activation(
                out=second[:], in_=results[2 * u + 1][:].indirect(l7[:]), func=COPY, scale=sp_sb[:, u, :]
            )
            met = keep.tile([P, E], F32, name="met%d" % u)
            nc.vector.tensor_sub(met[:], first[:], second[:])
            nc.sync.dma_start(out=out[P * u : P * (u + 1), :], in_=met[:])
